import numpy as np
import ml_dtypes


def mxq(x, axis, fmt="e4m3"):
    dtype, down = {"e4m3": (ml_dtypes.float8_e4m3fn, 7), "e5m2": (ml_dtypes.float8_e5m2, 14)}[fmt]
    v = np.moveaxis(np.asarray(x, np.float32).astype(ml_dtypes.bfloat16).astype(np.float64), axis, -1)
    blocks = v.reshape(v.shape[:-1] + (-1, 32))
    amax = np.abs(blocks).max(-1, keepdims=True)
    byte = np.maximum(np.where(amax > 0, np.frexp(amax)[1] - 1 + 127, 0) - down, 1)
    scale = np.exp2(byte - 127.0)
    codes = (blocks / scale).astype(np.float32).astype(dtype).astype(np.float64)
    return np.moveaxis((codes * scale).reshape(v.shape), -1, axis)


WIDE = False


def mx_kscale(k):
    if not WIDE:
        return np.ones(k)
    levels = np.array([10, -10, 5, -5, 0])
    if k % 512:
        return np.exp2(np.random.permutation(np.resize(levels, k // 32))).repeat(32)
    a = np.empty((k // 512, 16))
    for p in range(k // 512):
        a[p, :8] = np.random.permutation(np.resize(levels, 8))
        for g in range(8):
            far = levels[np.abs(levels - a[p, g]) >= 10]
            a[p, g + 8] = far[np.random.randint(len(far))]
    return np.exp2(a.ravel()).repeat(32)


def f64(x):
    return np.asarray(x).astype(np.float64)


def striped(idx):
    return np.tile(np.asarray(idx).reshape(-1, 16).T, (8, 1)).astype(np.uint16)


def unstriped(offs):
    return offs[:16].T.reshape(-1).astype(np.int64)


def striped8(idx):
    return np.asarray(idx).reshape(8, -1, 16).transpose(0, 2, 1).reshape(128, -1).astype(np.uint16)


def unstriped8(offs):
    return offs.reshape(8, 16, -1).transpose(0, 2, 1).reshape(8, -1).astype(np.int64)


def pick8(x, idx, run):
    r = np.arange(len(x))
    return x[r[:, None], idx[r % (8 * run) // run]]


E2M1 = np.array([0.0, 0.5, 1.0, 1.5, 2.0, 3.0, 4.0, 6.0, -0.0, -0.5, -1.0, -1.5, -2.0, -3.0, -4.0, -6.0])


def pack_weight(w, fmt):
    k, n = w.shape
    w = f64(np.asarray(w, np.float32).astype(ml_dtypes.bfloat16)).reshape(k // 32, 32, n)
    amax = np.abs(w).max(1)
    if fmt == "e4m3":
        byte = np.frexp(amax)[1] - 1 + 127 - 7
    else:
        mant, ex = np.frexp(amax / 6.0)
        byte = np.where(mant > 0.5, ex, ex - 1) + 127
    byte = np.clip(np.where(amax > 0, byte, 1), 1, 254)
    scaled = (w * np.exp2(127.0 - byte)[:, None, :]).reshape(k, n).astype(np.float32)
    by_word = np.ascontiguousarray(scaled.reshape(k // 512, 128, 4, n).transpose(0, 1, 3, 2))
    if fmt == "e4m3":
        words = by_word.astype(ml_dtypes.float8_e4m3fn).view(np.uint8)
    else:
        c = by_word.astype(ml_dtypes.float4_e2m1fn).view(np.uint8) & 0xF
        words = (c[..., 0::2] | (c[..., 1::2] << 4)).reshape(k // 512, 128, 2 * n)
    return np.ascontiguousarray(words), np.ascontiguousarray(byte.astype(np.uint8).reshape(k // 512, 16, n))


def unpack_weight(words, scales, fmt):
    g, _, n = scales.shape
    words = np.ascontiguousarray(words).reshape(g, 128, n, -1)
    if fmt == "e4m3":
        vals = words.view(ml_dtypes.float8_e4m3fn).astype(np.float64)
    else:
        nib = np.empty((g, 128, n, 4), np.uint8)
        nib[..., 0::2] = words & 0xF
        nib[..., 1::2] = words >> 4
        vals = E2M1[nib]
    vals = vals * np.repeat(np.exp2(scales.astype(np.float64) - 127.0), 8, axis=1)[..., None]
    return vals.transpose(0, 1, 3, 2).reshape(g * 512, n)


K, J, R, T, Z, M, S, C, N, V = 512, 512, 512, 2048, 512, 1024, 256, 512, 256, 1024


def setup_inputs():
    n = np.random.standard_normal
    idx = np.random.permutation(T)[:J]
    idx2 = np.random.permutation(M)[:J]
    idx3 = np.stack([np.random.permutation(J)[:S] for _ in range(8)])
    idx4 = np.stack([np.random.permutation(J)[:S] for _ in range(8)])
    idx5 = np.stack([np.random.permutation(C)[:S] for _ in range(8)])
    idx6 = np.random.permutation(V)[:N]
    fk = mx_kscale(K)
    fr = mx_kscale(R)
    fz = mx_kscale(Z)
    xtp = pack_weight(n((K, T)) * fk[:, None], "e2m1")
    wp = pack_weight(n((K, R)) * 1 / np.sqrt(K) / fk[:, None] * fr, "e4m3")
    xop = pack_weight(n((Z, M)) / fz[:, None], "e2m1")
    w2p = pack_weight(n((Z, R)) * 1 / np.sqrt(Z) * fz[:, None] * fr, "e4m3")
    vsp = pack_weight(n((R, V)) * 1 / np.sqrt(R) / fr[:, None], "e4m3")
    return {
        "xt_words": xtp[0],
        "xt_scales": xtp[1],
        "w_words": wp[0],
        "w_scales": wp[1],
        "xo_words": xop[0],
        "xo_scales": xop[1],
        "w2_words": w2p[0],
        "w2_scales": w2p[1],
        "sa": (np.random.uniform(0.5, 1.6, (R, 1))).astype(np.float32),
        "sb": (np.random.uniform(0.5, 1.6, (R, 1))).astype(np.float32),
        "vs_words": vsp[0],
        "vs_scales": vsp[1],
        "offs": striped(idx),
        "offs2": striped(idx2),
        "offs3": striped8(idx3),
        "offs4": striped8(idx4),
        "offs5": striped8(idx5),
        "offs6": striped(idx6),
    }


def reference(xt_words, xt_scales, w_words, w_scales, xo_words, xo_scales, w2_words, w2_scales, sa, sb, vs_words, vs_scales, offs, offs2, offs3, offs4, offs5, offs6):
    idx = unstriped(offs)
    idx2 = unstriped(offs2)
    idx3 = unstriped8(offs3)
    idx4 = unstriped8(offs4)
    idx5 = unstriped8(offs5)
    idx6 = unstriped(offs6)
    xtu = unpack_weight(xt_words, xt_scales, "e2m1")
    wu = unpack_weight(w_words, w_scales, "e4m3")
    xou = unpack_weight(xo_words, xo_scales, "e2m1")
    w2u = unpack_weight(w2_words, w2_scales, "e4m3")
    vsu = unpack_weight(vs_words, vs_scales, "e4m3")
    xtidxg = xtu[:, idx]
    a = wu.T @ xtidxg
    xoidx2g = xou[:, idx2]
    b = w2u.T @ xoidx2g
    h1 = np.maximum(pick8(a, idx3, 64) * f64(sa), pick8(b, idx4, 64) * f64(sb))
    hid = np.zeros((R, C))
    hid[np.arange(R)[:, None], idx5[np.arange(R) % 512 // 64]] = h1
    vsidx6g = vsu[:, idx6]
    hidq = mxq(hid, 0, "e4m3")
    y = vsidx6g.T @ hidq
    return y

@@ -1,0 +1,191 @@
+from contextlib import ExitStack
+
+import concourse.mybir as mybir
+
+F32 = mybir.dt.float32
+BF16 = mybir.dt.bfloat16
+I32 = mybir.dt.int32
+U32 = mybir.dt.uint32
+U16 = mybir.dt.uint16
+U8 = mybir.dt.uint8
+FP8X4 = mybir.dt.float8_e4m3fn_x4
+FP4X4 = mybir.dt.float4_e2m1fn_x4
+COPY = mybir.ActivationFunctionType.Copy
+MAX = mybir.AluOpType.max
+
+K, J, R, T, Z, M, S, C, N, V = 512, 512, 512, 2048, 512, 1024, 256, 512, 256, 1024
+P = 128
+PACK = 4
+HALF = C // 2
+FLOPS = 2 * (K * R * J + Z * R * J + R * N * C)
+
+
+def tile_picked_tokens_plain_two_pairpost_store_plain_kernel(
+    tc, xt_words, xt_scales, w_words, w_scales, xo_words, xo_scales, w2_words, w2_scales, sa, sb,
+    vs_words, vs_scales, offs, offs2, offs3, offs4, offs5, offs6, out,
+):
+    nc = tc.nc
+    with ExitStack() as ctx:
+        keep = ctx.enter_context(tc.tile_pool(name="keep", bufs=1))
+        psum = ctx.enter_context(tc.psum_pool(name="psum", bufs=4))
+
+        def sbuf(name, width, dtype):
+            return keep.tile([P, width], dtype, name=name, align_bytes=64)
+
+        def zeroed_plane(name, width):
+            plane = sbuf(name, width, U8)
+            nc.vector.memset(plane[:].bitcast(I32), 0)
+            return plane
+
+        def load_scales(plane, scales):
+            for q in range(4):
+                nc.sync.dma_start(
+                    out=plane[32 * q : 32 * q + 4, :].bitcast(I32),
+                    in_=scales[0, 4 * q : 4 * q + 4, :].bitcast(I32),
+                )
+
+        def load_list(name, source, entries):
+            offsets = sbuf(name, entries // 16, U16)
+            nc.sync.dma_start(offsets[:], source)
+            return offsets
+
+        def load_fp4_words(name, words, width):
+            tile = sbuf(name, width, U16)
+            nc.sync.dma_start(out=tile[:].bitcast(I32), in_=words[0].bitcast(I32))
+            return tile
+
+        def load_fp8_words(name, words, width):
+            tile = sbuf(name, width, U32)
+            nc.sync.dma_start(out=tile[:].bitcast(I32), in_=words[0].rearrange("p n t -> p (n t)").bitcast(I32))
+            return tile
+
+        def load_gain(name, gain):
+            tile = sbuf(name, PACK, F32)
+            nc.gpsimd.dma_start(out=tile[:], in_=gain.rearrange("(p t) o -> p (t o)", t=PACK))
+            return tile
+
+        def gather(name, window, offsets, entries, dtype):
+            picked = sbuf(name, entries, dtype)
+            nc.vector.tensor_copy(picked[:], window[:].indirect(offsets[:]))
+            return picked
+
+        def deal(name, words, plane):
+            dealt_words = sbuf(name + "_dealt_words", R, U32)
+            dealt_plane = sbuf(name + "_dealt_scales", R, U8)
+            nc.scalar.copy(
+                out=dealt_words[:].rearrange("p (t m) -> p m t", t=PACK),
+                in_=words[:].rearrange("p (m t) -> p m t", t=PACK),
+            )
+            nc.gpsimd.tensor_copy(
+                out=dealt_plane[:].rearrange("p (t m) -> p t m", t=PACK),
+                in_=plane[:].rearrange("p (m t) -> p t m", t=PACK),
+            )
+            return dealt_words, dealt_plane
+
+        def product(tag, t, weights, picked_words, picked_scales):
+            bank = psum.tile([P, J], F32, name=tag, tag=tag)
+            cols = slice(P * t, P * (t + 1))
+            nc.tensor.matmul_mx(
+                out=bank[:], lhsT=weights[0][:, cols].bitcast(FP8X4), lhsT_scale=weights[1][:, cols],
+                rhs=picked_words[:].bitcast(FP4X4), rhs_scale=picked_scales[:], start=True, stop=True,
+            )
+            return bank
+
+        xo_plane = zeroed_plane("xo_plane", M)
+        w2_plane = zeroed_plane("w2_plane", R)
+        xt_plane = zeroed_plane("xt_plane", T)
+        w_plane = zeroed_plane("w_plane", R)
+        vs_plane = zeroed_plane("vs_plane", V)
+        page = []
+        for t in range(PACK):
+            tile = sbuf("page%d" % t, C, F32)
+            nc.vector.memset(tile[:], 0.0)
+            page.append(tile)
+
+        gain_b = load_gain("gain_b", sb)
+        gain_a = load_gain("gain_a", sa)
+        xo_tile = load_fp4_words("xo_tile", xo_words, M)
+        list2 = load_list("list2", offs2, J)
+        load_scales(xo_plane, xo_scales)
+        list1 = load_list("list1", offs, J)
+        xt_tile = load_fp4_words("xt_tile", xt_words, T)
+        w2_tile = load_fp8_words("w2_tile", w2_words, R)
+        load_scales(w2_plane, w2_scales)
+        load_scales(xt_plane, xt_scales)
+        w_tile = load_fp8_words("w_tile", w_words, R)
+        load_scales(w_plane, w_scales)
+        list4 = load_list("list4", offs4, S)
+        list3 = load_list("list3", offs3, S)
+        list5 = load_list("list5", offs5, S)
+        list6 = load_list("list6", offs6, N)
+        vs_tile = load_fp8_words("vs_tile", vs_words, V)
+        load_scales(vs_plane, vs_scales)
+
+        xo_picked = gather("xo_picked", xo_tile, list2, J, U16)
+        xo_picked_scales = gather("xo_picked_scales", xo_plane, list2, J, U8)
+        w2_dealt = deal("w2", w2_tile, w2_plane)
+        b_banks = [product("b", t, w2_dealt, xo_picked, xo_picked_scales) for t in range(PACK)]
+        xt_picked = gather("xt_picked", xt_tile, list1, J, U16)
+        xt_picked_scales = gather("xt_picked_scales", xt_plane, list1, J, U8)
+        w_dealt = deal("w", w_tile, w_plane)
+        a_banks = [product("a", t, w_dealt, xt_picked, xt_picked_scales) for t in range(PACK)]
+
+        def leave_bank(name, bank, on_scalar):
+            rows = sbuf(name, J, F32)
+            if on_scalar:
+                nc.scalar.activation(out=rows[:], in_=bank[:], func=COPY)
+            else:
+                nc.vector.tensor_copy(out=rows[:], in_=bank[:])
+            return rows
+
+        def fetch(name, rows, offsets, gain, t):
+            fetched = sbuf(name, S, F32)
+            nc.scalar.activation(
+                out=fetched[:], in_=rows[:].indirect(offsets[:]), func=COPY, scale=gain[:, t : t + 1]
+            )
+            return fetched
+
+        woven = keep.tile([P, C, PACK], BF16, name="woven", align_bytes=64)
+        b_fetched = {}
+        for t in range(2):
+            b_fetched[t] = fetch("bf%d" % t, leave_bank("b%d" % t, b_banks[t], True), list4, gain_b, t)
+        for t in range(PACK):
+            a_rows = leave_bank("a%d" % t, a_banks[t], False)
+            if t >= 2:
+                b_fetched[t] = fetch("bf%d" % t, leave_bank("b%d" % t, b_banks[t], False), list4, gain_b, t)
+            a_fetched = fetch("af%d" % t, a_rows, list3, gain_a, t)
+            larger = sbuf("larger%d" % t, S, F32)
+            nc.vector.tensor_tensor(larger[:], a_fetched[:], b_fetched[t][:], MAX)
+            nc.scalar.activation(out=page[t][:].indirect(list5[:]), in_=larger[:], func=COPY)
+            if t == 1:
+                vs_picked = gather("vs_picked", vs_tile, list6, N, U32)
+                vs_picked_scales = gather("vs_picked_scales", vs_plane, list6, N, U8)
+            if t < PACK - 1:
+                nc.vector.tensor_copy(out=woven[:, :, t], in_=page[t][:])
+
+        codes = sbuf("codes", C, U32)
+        code_scales = sbuf("code_scales", C, U8)
+        for h in range(2):
+            cols = slice(HALF * h, HALF * (h + 1))
+            nc.vector.tensor_copy(out=woven[:, cols, PACK - 1], in_=page[PACK - 1][:, cols])
+        for h in range(2):
+            cols = slice(HALF * h, HALF * (h + 1))
+            nc.vector.quantize_mx(
+                out=codes[:, cols].bitcast(FP8X4), scales=code_scales[:, cols],
+                in_=woven[:, cols, :].rearrange("p c t -> p (c t)"),
+            )
+        for h in range(2):
+            cols = slice(HALF * h, HALF * (h + 1))
+            bank = psum.tile([P, 2, HALF], F32, name="b", tag="b")
+            for m in range(N // P):
+                rows = slice(P * m, P * (m + 1))
+                nc.tensor.matmul_mx(
+                    out=bank[:, m, :], lhsT=vs_picked[:, rows].bitcast(FP8X4), lhsT_scale=vs_picked_scales[:, rows],
+                    rhs=codes[:, cols].bitcast(FP8X4), rhs_scale=code_scales[:, cols], start=True, stop=True,
+                )
+            result = keep.tile([P, 2, HALF], F32, name="result%d" % h)
+            if h == 0:
+                nc.scalar.activation(out=result[:], in_=bank[:], func=COPY)
+            else:
+                nc.vector.tensor_copy(out=result[:], in_=bank[:])
+            nc.sync.dma_start(out=out[:, cols].rearrange("(m p) c -> p m c", p=P), in_=result[:])

@@ -16,7 +16,9 @@ MAX = mybir.AluOpType.max
 K, J, R, T, Z, M, S, C, N, V = 512, 512, 512, 2048, 512, 1024, 256, 512, 256, 1024
 P = 128
 PACK = 4
-HALF = C // 2
+ORDER = (2, 0, 1, 3)
+PIECES = 4
+PIECE = C // PIECES
 FLOPS = 2 * (K * R * J + Z * R * J + R * N * C)
 
 
@@ -27,22 +29,31 @@ def tile_picked_tokens_plain_two_pairpost_store_plain_kernel(
     nc = tc.nc
     with ExitStack() as ctx:
         keep = ctx.enter_context(tc.tile_pool(name="keep", bufs=1))
-        psum = ctx.enter_context(tc.psum_pool(name="psum", bufs=4))
+        psum = ctx.enter_context(tc.psum_pool(name="psum", bufs=8))
 
-        def sbuf(name, width, dtype):
-            return keep.tile([P, width], dtype, name=name, align_bytes=64)
+        def sbuf(name, width, dtype, tag=None):
+            return keep.tile([P, width], dtype, name=name, tag=tag or name, align_bytes=64)
 
         def zeroed_plane(name, width):
             plane = sbuf(name, width, U8)
             nc.vector.memset(plane[:].bitcast(I32), 0)
             return plane
 
-        def load_scales(plane, scales):
-            for q in range(4):
+        def load_scales(plane, scales, quadrants=range(4)):
+            for q in quadrants:
                 nc.sync.dma_start(
                     out=plane[32 * q : 32 * q + 4, :].bitcast(I32),
                     in_=scales[0, 4 * q : 4 * q + 4, :].bitcast(I32),
                 )
+
+        def folded_plane(plane):
+            nc.vector.memset(plane[:].bitcast(I32), 0)
+            return plane
+
+        def load_folded_scales(plane, scales):
+            rows = scales[0].rearrange("(h q j) n -> q j h n", h=2, q=2)
+            for q in range(2):
+                nc.sync.dma_start(out=plane[32 * q : 32 * q + 4].bitcast(I32), in_=rows[q].bitcast(I32))
 
         def load_list(name, source, entries):
             offsets = sbuf(name, entries // 16, U16)
@@ -61,82 +72,71 @@ def tile_picked_tokens_plain_two_pairpost_store_plain_kernel(
 
         def load_gain(name, gain):
             tile = sbuf(name, PACK, F32)
-            nc.gpsimd.dma_start(out=tile[:], in_=gain.rearrange("(p t) o -> p (t o)", t=PACK))
+            nc.sync.dma_start(out=tile[:], in_=gain.rearrange("(p t) o -> p (t o)", t=PACK))
             return tile
 
-        def gather(name, window, offsets, entries, dtype):
-            picked = sbuf(name, entries, dtype)
+        def gather(name, window, offsets, entries, dtype, tag=None):
+            picked = sbuf(name, entries, dtype, tag)
             nc.vector.tensor_copy(picked[:], window[:].indirect(offsets[:]))
             return picked
 
-        def deal(name, words, plane):
+        def deal_words(name, words):
             dealt_words = sbuf(name + "_dealt_words", R, U32)
-            dealt_plane = sbuf(name + "_dealt_scales", R, U8)
             nc.scalar.copy(
                 out=dealt_words[:].rearrange("p (t m) -> p m t", t=PACK),
                 in_=words[:].rearrange("p (m t) -> p m t", t=PACK),
             )
-            nc.gpsimd.tensor_copy(
-                out=dealt_plane[:].rearrange("p (t m) -> p t m", t=PACK),
-                in_=plane[:].rearrange("p (m t) -> p t m", t=PACK),
-            )
-            return dealt_words, dealt_plane
+            return dealt_words
 
-        def product(tag, t, weights, picked_words, picked_scales):
-            bank = psum.tile([P, J], F32, name=tag, tag=tag)
+        def deal_scales(name, plane):
+            dealt_plane = sbuf(name + "_dealt_scales", R, U8)
+            nc.vector.tensor_copy(out=plane[64:128, 0, :].bitcast(I32), in_=plane[0:64, 1, :].bitcast(I32))
+            nc.vector.tensor_copy(
+                out=dealt_plane[:].rearrange("p (t m) -> p t m", t=PACK),
+                in_=plane[:, 0, :].rearrange("p (m t) -> p t m", t=PACK),
+            )
+            return dealt_plane
+
+        def product(t, weights, picked_words, picked_scales):
+            bank = psum.tile([P, picked_scales.shape[1]], F32, name="bank")
             cols = slice(P * t, P * (t + 1))
             nc.tensor.matmul_mx(
                 out=bank[:], lhsT=weights[0][:, cols].bitcast(FP8X4), lhsT_scale=weights[1][:, cols],
-                rhs=picked_words[:].bitcast(FP4X4), rhs_scale=picked_scales[:], start=True, stop=True,
+                rhs=picked_words.bitcast(FP4X4), rhs_scale=picked_scales, start=True, stop=True,
             )
             return bank
 
+        w2_plane = folded_plane(keep.tile([P, 2, R], U8, name="w2_plane", align_bytes=64))
         xo_plane = zeroed_plane("xo_plane", M)
-        w2_plane = zeroed_plane("w2_plane", R)
         xt_plane = zeroed_plane("xt_plane", T)
-        w_plane = zeroed_plane("w_plane", R)
+        w_plane = folded_plane(keep.tile([P, 2, R], U8, name="w_plane", tag="w_plane", align_bytes=64))
         vs_plane = zeroed_plane("vs_plane", V)
-        page = []
-        for t in range(PACK):
-            tile = sbuf("page%d" % t, C, F32)
-            nc.vector.memset(tile[:], 0.0)
-            page.append(tile)
 
-        gain_b = load_gain("gain_b", sb)
-        gain_a = load_gain("gain_a", sa)
         xo_tile = load_fp4_words("xo_tile", xo_words, M)
         list2 = load_list("list2", offs2, J)
-        load_scales(xo_plane, xo_scales)
-        list1 = load_list("list1", offs, J)
-        xt_tile = load_fp4_words("xt_tile", xt_words, T)
         w2_tile = load_fp8_words("w2_tile", w2_words, R)
-        load_scales(w2_plane, w2_scales)
-        load_scales(xt_plane, xt_scales)
+        load_folded_scales(w2_plane, w2_scales)
+        load_scales(xo_plane, xo_scales)
         w_tile = load_fp8_words("w_tile", w_words, R)
-        load_scales(w_plane, w_scales)
+        list1 = load_list("list1", offs, J)
+        load_folded_scales(w_plane, w_scales)
+        load_scales(xt_plane, xt_scales, (0, 1))
+        xt_tile = load_fp4_words("xt_tile", xt_words, T)
+        load_scales(xt_plane, xt_scales, (2, 3))
         list4 = load_list("list4", offs4, S)
+        gain_b = load_gain("gain_b", sb)
         list3 = load_list("list3", offs3, S)
-        list5 = load_list("list5", offs5, S)
+        gain_a = load_gain("gain_a", sa)
         list6 = load_list("list6", offs6, N)
         vs_tile = load_fp8_words("vs_tile", vs_words, V)
         load_scales(vs_plane, vs_scales)
+        list5 = load_list("list5", offs5, S)
 
-        xo_picked = gather("xo_picked", xo_tile, list2, J, U16)
-        xo_picked_scales = gather("xo_picked_scales", xo_plane, list2, J, U8)
-        w2_dealt = deal("w2", w2_tile, w2_plane)
-        b_banks = [product("b", t, w2_dealt, xo_picked, xo_picked_scales) for t in range(PACK)]
-        xt_picked = gather("xt_picked", xt_tile, list1, J, U16)
-        xt_picked_scales = gather("xt_picked_scales", xt_plane, list1, J, U8)
-        w_dealt = deal("w", w_tile, w_plane)
-        a_banks = [product("a", t, w_dealt, xt_picked, xt_picked_scales) for t in range(PACK)]
-
-        def leave_bank(name, bank, on_scalar):
-            rows = sbuf(name, J, F32)
+        def leave_bank(rows, bank, on_scalar):
             if on_scalar:
-                nc.scalar.activation(out=rows[:], in_=bank[:], func=COPY)
+                nc.scalar.activation(out=rows, in_=bank[:], func=COPY)
             else:
-                nc.vector.tensor_copy(out=rows[:], in_=bank[:])
-            return rows
+                nc.vector.tensor_copy(out=rows, in_=bank[:])
 
         def fetch(name, rows, offsets, gain, t):
             fetched = sbuf(name, S, F32)
@@ -145,47 +145,99 @@ def tile_picked_tokens_plain_two_pairpost_store_plain_kernel(
             )
             return fetched
 
-        woven = keep.tile([P, C, PACK], BF16, name="woven", align_bytes=64)
-        b_fetched = {}
-        for t in range(2):
-            b_fetched[t] = fetch("bf%d" % t, leave_bank("b%d" % t, b_banks[t], True), list4, gain_b, t)
-        for t in range(PACK):
-            a_rows = leave_bank("a%d" % t, a_banks[t], False)
-            if t >= 2:
-                b_fetched[t] = fetch("bf%d" % t, leave_bank("b%d" % t, b_banks[t], False), list4, gain_b, t)
-            a_fetched = fetch("af%d" % t, a_rows, list3, gain_a, t)
-            larger = sbuf("larger%d" % t, S, F32)
-            nc.vector.tensor_tensor(larger[:], a_fetched[:], b_fetched[t][:], MAX)
+        w2_dealt_words = deal_words("w2", w2_tile)
+        w_dealt_words = deal_words("w", w_tile)
+        xo_picked = gather("xo_picked", xo_tile, list2, J, U16)
+        w2_dealt = (w2_dealt_words, deal_scales("w2", w2_plane))
+
+        def halves(name, plane, offsets):
+            picked = sbuf(name, J, U8)
+            for half in range(2):
+                slots = slice(J // 2 * half, J // 2 * (half + 1))
+                nc.vector.tensor_copy(
+                    picked[:, slots], plane[:].indirect(offsets[:, slots.start // 16 : slots.stop // 16])
+                )
+            return picked
+
+        def product_in_halves(tiles, rows, weights, words, scales, on_scalar):
+            for half in range(2):
+                slots = slice(J // 2 * half, J // 2 * (half + 1))
+                for t in tiles:
+                    leave_bank(rows[t][:, slots], product(t, weights, words[:, slots], scales[:, slots]), on_scalar)
+
+        first, second, third, last = ORDER
+        xo_picked_scales = halves("xo_picked_scales", xo_plane, list2)
+        b_rows = {t: sbuf("b%d" % t, J, F32) for t in (first, second, third)}
+        product_in_halves((first, second), b_rows, w2_dealt, xo_picked, xo_picked_scales, True)
+        leave_bank(b_rows[third][:], product(third, w2_dealt, xo_picked[:], xo_picked_scales[:]), True)
+        last_b_bank = product(last, w2_dealt, xo_picked[:], xo_picked_scales[:])
+        xt_picked = gather("xt_picked", xt_tile, list1, J, U16)
+        w_dealt = (w_dealt_words, deal_scales("w", w_plane))
+        xt_picked_scales = halves("xt_picked_scales", xt_plane, list1)
+        b_rows[last] = sbuf("b%d" % last, J, F32, "xt_plane")
+        leave_bank(b_rows[last][:], last_b_bank, False)
+        b_fetched = {t: fetch("bf%d" % t, b_rows[t], list4, gain_b, t) for t in ORDER}
+        a_rows = {t: sbuf("a%d" % t, J, F32) for t in ORDER}
+        product_in_halves((first,), a_rows, w_dealt, xt_picked, xt_picked_scales, False)
+        for t in (second, third, last):
+            leave_bank(a_rows[t][:], product(t, w_dealt, xt_picked[:], xt_picked_scales[:]), False)
+        a_fetched = {t: fetch("af%d" % t, a_rows[t], list3, gain_a, t) for t in ORDER}
+        page = {}
+        for t in ORDER:
+            page[t] = sbuf("page%d" % t, C, F32, "a%d" % t)
+            nc.gpsimd.memset(page[t][:], 0.0)
+
+        def put(t, tag):
+            larger = sbuf("larger%d" % t, S, F32, tag)
+            nc.vector.tensor_tensor(larger[:], a_fetched[t][:], b_fetched[t][:], MAX)
             nc.scalar.activation(out=page[t][:].indirect(list5[:]), in_=larger[:], func=COPY)
-            if t == 1:
-                vs_picked = gather("vs_picked", vs_tile, list6, N, U32)
-                vs_picked_scales = gather("vs_picked_scales", vs_plane, list6, N, U8)
-            if t < PACK - 1:
-                nc.vector.tensor_copy(out=woven[:, :, t], in_=page[t][:])
+
+        for t in (first, second, third):
+            put(t, None)
+        vs_picked_scales = gather("vs_picked_scales", vs_plane, list6, N, U8, "af%d" % third)
+        vs_picked = gather("vs_picked", vs_tile, list6, N, U32, "vs_plane")
+        woven = keep.tile([P, C, PACK], BF16, name="woven", tag="vs_tile", align_bytes=64)
+        nc.vector.tensor_copy(out=woven[:, :, first], in_=page[first][:])
+        put(last, "a%d" % first)
+        for t in (second, third):
+            nc.vector.tensor_copy(out=woven[:, :, t], in_=page[t][:])
 
         codes = sbuf("codes", C, U32)
         code_scales = sbuf("code_scales", C, U8)
-        for h in range(2):
-            cols = slice(HALF * h, HALF * (h + 1))
-            nc.vector.tensor_copy(out=woven[:, cols, PACK - 1], in_=page[PACK - 1][:, cols])
-        for h in range(2):
-            cols = slice(HALF * h, HALF * (h + 1))
+
+        def weave_last(h):
+            cols = slice(PIECE * h, PIECE * (h + 1))
+            if h < PIECES // 2:
+                nc.vector.tensor_copy(out=woven[:, cols, PACK - 1], in_=page[PACK - 1][:, cols])
+            else:
+                nc.scalar.copy(out=woven[:, cols, PACK - 1], in_=page[PACK - 1][:, cols])
+
+        def finish(h):
+            cols = slice(PIECE * h, PIECE * (h + 1))
             nc.vector.quantize_mx(
                 out=codes[:, cols].bitcast(FP8X4), scales=code_scales[:, cols],
                 in_=woven[:, cols, :].rearrange("p c t -> p (c t)"),
             )
-        for h in range(2):
-            cols = slice(HALF * h, HALF * (h + 1))
-            bank = psum.tile([P, 2, HALF], F32, name="b", tag="b")
+            bank = psum.tile([P, N // P, PIECE], F32, name="bank")
             for m in range(N // P):
                 rows = slice(P * m, P * (m + 1))
                 nc.tensor.matmul_mx(
                     out=bank[:, m, :], lhsT=vs_picked[:, rows].bitcast(FP8X4), lhsT_scale=vs_picked_scales[:, rows],
                     rhs=codes[:, cols].bitcast(FP8X4), rhs_scale=code_scales[:, cols], start=True, stop=True,
                 )
-            result = keep.tile([P, 2, HALF], F32, name="result%d" % h)
-            if h == 0:
-                nc.scalar.activation(out=result[:], in_=bank[:], func=COPY)
-            else:
-                nc.vector.tensor_copy(out=result[:], in_=bank[:])
+            return bank
+
+        def store(h, bank):
+            cols = slice(PIECE * h, PIECE * (h + 1))
+            result = keep.tile([P, N // P, PIECE], F32, name="result%d" % h)
+            leave_bank(result[:], bank, h < PIECES - 1)
             nc.sync.dma_start(out=out[:, cols].rearrange("(m p) c -> p m c", p=P), in_=result[:])
+
+        weave_last(0)
+        banks = []
+        for h in range(PIECES):
+            if h + 1 < PIECES:
+                weave_last(h + 1)
+            banks.append(finish(h))
+        for h in range(PIECES):
+            store(h, banks[h])

@@ -65,9 +65,9 @@ def tile_picked_tokens_plain_two_pairpost_store_plain_kernel(
             nc.sync.dma_start(out=tile[:].bitcast(I32), in_=words[0].bitcast(I32))
             return tile
 
-        def load_fp8_words(name, words, width):
+        def load_fp8_words(name, words, width, queue):
             tile = sbuf(name, width, U32)
-            nc.sync.dma_start(out=tile[:].bitcast(I32), in_=words[0].rearrange("p n t -> p (n t)").bitcast(I32))
+            queue.dma_start(out=tile[:].bitcast(I32), in_=words[0].rearrange("p n t -> p (n t)").bitcast(I32))
             return tile
 
         def load_gain(name, gain):
@@ -113,22 +113,22 @@ def tile_picked_tokens_plain_two_pairpost_store_plain_kernel(
         vs_plane = zeroed_plane("vs_plane", V)
 
         xo_tile = load_fp4_words("xo_tile", xo_words, M)
-        list2 = load_list("list2", offs2, J)
-        w2_tile = load_fp8_words("w2_tile", w2_words, R)
+        w2_tile = load_fp8_words("w2_tile", w2_words, R, nc.gpsimd)
         load_folded_scales(w2_plane, w2_scales)
         load_scales(xo_plane, xo_scales)
-        w_tile = load_fp8_words("w_tile", w_words, R)
+        list2 = load_list("list2", offs2, J)
+        w_tile = load_fp8_words("w_tile", w_words, R, nc.sync)
         list1 = load_list("list1", offs, J)
         load_folded_scales(w_plane, w_scales)
-        load_scales(xt_plane, xt_scales, (0, 1))
+        load_scales(xt_plane, xt_scales, (0, 1, 2))
         xt_tile = load_fp4_words("xt_tile", xt_words, T)
-        load_scales(xt_plane, xt_scales, (2, 3))
+        load_scales(xt_plane, xt_scales, (3,))
         list4 = load_list("list4", offs4, S)
         gain_b = load_gain("gain_b", sb)
         list3 = load_list("list3", offs3, S)
         gain_a = load_gain("gain_a", sa)
         list6 = load_list("list6", offs6, N)
-        vs_tile = load_fp8_words("vs_tile", vs_words, V)
+        vs_tile = load_fp8_words("vs_tile", vs_words, V, nc.sync)
         load_scales(vs_plane, vs_scales)
         list5 = load_list("list5", offs5, S)
 
@@ -147,38 +147,33 @@ def tile_picked_tokens_plain_two_pairpost_store_plain_kernel(
 
         w2_dealt_words = deal_words("w2", w2_tile)
         w_dealt_words = deal_words("w", w_tile)
-        xo_picked = gather("xo_picked", xo_tile, list2, J, U16)
-        w2_dealt = (w2_dealt_words, deal_scales("w2", w2_plane))
-
-        def halves(name, plane, offsets):
-            picked = sbuf(name, J, U8)
-            for half in range(2):
-                slots = slice(J // 2 * half, J // 2 * (half + 1))
-                nc.vector.tensor_copy(
-                    picked[:, slots], plane[:].indirect(offsets[:, slots.start // 16 : slots.stop // 16])
-                )
-            return picked
-
-        def product_in_halves(tiles, rows, weights, words, scales, on_scalar):
-            for half in range(2):
-                slots = slice(J // 2 * half, J // 2 * (half + 1))
-                for t in tiles:
-                    leave_bank(rows[t][:, slots], product(t, weights, words[:, slots], scales[:, slots]), on_scalar)
-
         first, second, third, last = ORDER
-        xo_picked_scales = halves("xo_picked_scales", xo_plane, list2)
-        b_rows = {t: sbuf("b%d" % t, J, F32) for t in (first, second, third)}
-        product_in_halves((first, second), b_rows, w2_dealt, xo_picked, xo_picked_scales, True)
-        leave_bank(b_rows[third][:], product(third, w2_dealt, xo_picked[:], xo_picked_scales[:]), True)
-        last_b_bank = product(last, w2_dealt, xo_picked[:], xo_picked_scales[:])
-        xt_picked = gather("xt_picked", xt_tile, list1, J, U16)
+        half_slots = [slice(J // 2 * half, J // 2 * (half + 1)) for half in range(2)]
+
+        def gather_slots(picked, window, offsets, slots):
+            nc.vector.tensor_copy(picked[:, slots], window[:].indirect(offsets[:, slots.start // 16 : slots.stop // 16]))
+
+        xo_picked = sbuf("xo_picked", J, U16)
+        xo_picked_scales = sbuf("xo_picked_scales", J, U8)
+        b_rows = {t: sbuf("b%d" % t, J, F32) for t in ORDER}
+        w2_dealt = (w2_dealt_words, deal_scales("w2", w2_plane))
+        for slots in half_slots:
+            gather_slots(xo_picked, xo_tile, list2, slots)
+            gather_slots(xo_picked_scales, xo_plane, list2, slots)
+        for slots in half_slots:
+            for t in ORDER:
+                bank = product(t, w2_dealt, xo_picked[:, slots], xo_picked_scales[:, slots])
+                leave_bank(b_rows[t][:, slots], bank, True)
         w_dealt = (w_dealt_words, deal_scales("w", w_plane))
-        xt_picked_scales = halves("xt_picked_scales", xt_plane, list1)
-        b_rows[last] = sbuf("b%d" % last, J, F32, "xt_plane")
-        leave_bank(b_rows[last][:], last_b_bank, False)
+        xt_picked = gather("xt_picked", xt_tile, list1, J, U16)
+        xt_picked_scales = sbuf("xt_picked_scales", J, U8)
+        for slots in half_slots:
+            gather_slots(xt_picked_scales, xt_plane, list1, slots)
         b_fetched = {t: fetch("bf%d" % t, b_rows[t], list4, gain_b, t) for t in ORDER}
         a_rows = {t: sbuf("a%d" % t, J, F32) for t in ORDER}
-        product_in_halves((first,), a_rows, w_dealt, xt_picked, xt_picked_scales, False)
+        for slots in half_slots:
+            bank = product(first, w_dealt, xt_picked[:, slots], xt_picked_scales[:, slots])
+            leave_bank(a_rows[first][:, slots], bank, False)
         for t in (second, third, last):
             leave_bank(a_rows[t][:], product(t, w_dealt, xt_picked[:], xt_picked_scales[:]), False)
         a_fetched = {t: fetch("af%d" % t, a_rows[t], list3, gain_a, t) for t in ORDER}

from contextlib import ExitStack

import concourse.mybir as mybir

F32 = mybir.dt.float32
BF16 = mybir.dt.bfloat16
I32 = mybir.dt.int32
U32 = mybir.dt.uint32
U16 = mybir.dt.uint16
U8 = mybir.dt.uint8
FP8X4 = mybir.dt.float8_e4m3fn_x4
FP4X4 = mybir.dt.float4_e2m1fn_x4
COPY = mybir.ActivationFunctionType.Copy
MAX = mybir.AluOpType.max

K, J, R, T, Z, M, S, C, N, V = 512, 512, 512, 2048, 512, 1024, 256, 512, 256, 1024
P = 128
PACK = 4
ORDER = (2, 0, 1, 3)
PIECES = 4
PIECE = C // PIECES
FLOPS = 2 * (K * R * J + Z * R * J + R * N * C)


def tile_picked_tokens_plain_two_pairpost_store_plain_kernel(
    tc, xt_words, xt_scales, w_words, w_scales, xo_words, xo_scales, w2_words, w2_scales, sa, sb,
    vs_words, vs_scales, offs, offs2, offs3, offs4, offs5, offs6, out,
):
    nc = tc.nc
    with ExitStack() as ctx:
        keep = ctx.enter_context(tc.tile_pool(name="keep", bufs=1))
        psum = ctx.enter_context(tc.psum_pool(name="psum", bufs=8))

        def sbuf(name, width, dtype, tag=None):
            return keep.tile([P, width], dtype, name=name, tag=tag or name, align_bytes=64)

        def zeroed_plane(name, width):
            plane = sbuf(name, width, U8)
            nc.vector.memset(plane[:].bitcast(I32), 0)
            return plane

        def load_scales(plane, scales, quadrants=range(4)):
            for q in quadrants:
                nc.sync.dma_start(
                    out=plane[32 * q : 32 * q + 4, :].bitcast(I32),
                    in_=scales[0, 4 * q : 4 * q + 4, :].bitcast(I32),
                )

        def folded_plane(plane):
            nc.vector.memset(plane[:].bitcast(I32), 0)
            return plane

        def load_folded_scales(plane, scales):
            rows = scales[0].rearrange("(h q j) n -> q j h n", h=2, q=2)
            for q in range(2):
                nc.sync.dma_start(out=plane[32 * q : 32 * q + 4].bitcast(I32), in_=rows[q].bitcast(I32))

        def load_list(name, source, entries):
            offsets = sbuf(name, entries // 16, U16)
            nc.sync.dma_start(offsets[:], source)
            return offsets

        def load_fp4_words(name, words, width):
            tile = sbuf(name, width, U16)
            nc.sync.dma_start(out=tile[:].bitcast(I32), in_=words[0].bitcast(I32))
            return tile

        def load_fp8_words(name, words, width, queue):
            tile = sbuf(name, width, U32)
            queue.dma_start(out=tile[:].bitcast(I32), in_=words[0].rearrange("p n t -> p (n t)").bitcast(I32))
            return tile

        def load_gain(name, gain):
            tile = sbuf(name, PACK, F32)
            nc.sync.dma_start(out=tile[:], in_=gain.rearrange("(p t) o -> p (t o)", t=PACK))
            return tile

        def gather(name, window, offsets, entries, dtype, tag=None):
            picked = sbuf(name, entries, dtype, tag)
            nc.vector.tensor_copy(picked[:], window[:].indirect(offsets[:]))
            return picked

        def deal_words(name, words):
            dealt_words = sbuf(name + "_dealt_words", R, U32)
            nc.scalar.copy(
                out=dealt_words[:].rearrange("p (t m) -> p m t", t=PACK),
                in_=words[:].rearrange("p (m t) -> p m t", t=PACK),
            )
            return dealt_words

        def deal_scales(name, plane):
            dealt_plane = sbuf(name + "_dealt_scales", R, U8)
            nc.vector.tensor_copy(out=plane[64:128, 0, :].bitcast(I32), in_=plane[0:64, 1, :].bitcast(I32))
            nc.vector.tensor_copy(
                out=dealt_plane[:].rearrange("p (t m) -> p t m", t=PACK),
                in_=plane[:, 0, :].rearrange("p (m t) -> p t m", t=PACK),
            )
            return dealt_plane

        def product(t, weights, picked_words, picked_scales):
            bank = psum.tile([P, picked_scales.shape[1]], F32, name="bank")
            cols = slice(P * t, P * (t + 1))
            nc.tensor.matmul_mx(
                out=bank[:], lhsT=weights[0][:, cols].bitcast(FP8X4), lhsT_scale=weights[1][:, cols],
                rhs=picked_words.bitcast(FP4X4), rhs_scale=picked_scales, start=True, stop=True,
            )
            return bank

        w2_plane = folded_plane(keep.tile([P, 2, R], U8, name="w2_plane", align_bytes=64))
        xo_plane = zeroed_plane("xo_plane", M)
        xt_plane = zeroed_plane("xt_plane", T)
        w_plane = folded_plane(keep.tile([P, 2, R], U8, name="w_plane", tag="w_plane", align_bytes=64))
        vs_plane = zeroed_plane("vs_plane", V)

        xo_tile = load_fp4_words("xo_tile", xo_words, M)
        w2_tile = load_fp8_words("w2_tile", w2_words, R, nc.gpsimd)
        load_folded_scales(w2_plane, w2_scales)
        load_scales(xo_plane, xo_scales)
        list2 = load_list("list2", offs2, J)
        w_tile = load_fp8_words("w_tile", w_words, R, nc.sync)
        list1 = load_list("list1", offs, J)
        load_folded_scales(w_plane, w_scales)
        load_scales(xt_plane, xt_scales, (0, 1, 2))
        xt_tile = load_fp4_words("xt_tile", xt_words, T)
        load_scales(xt_plane, xt_scales, (3,))
        list4 = load_list("list4", offs4, S)
        gain_b = load_gain("gain_b", sb)
        list3 = load_list("list3", offs3, S)
        gain_a = load_gain("gain_a", sa)
        list6 = load_list("list6", offs6, N)
        vs_tile = load_fp8_words("vs_tile", vs_words, V, nc.sync)
        load_scales(vs_plane, vs_scales)
        list5 = load_list("list5", offs5, S)

        def leave_bank(rows, bank, on_scalar):
            if on_scalar:
                nc.scalar.activation(out=rows, in_=bank[:], func=COPY)
            else:
                nc.vector.tensor_copy(out=rows, in_=bank[:])

        def fetch(name, rows, offsets, gain, t):
            fetched = sbuf(name, S, F32)
            nc.scalar.activation(
                out=fetched[:], in_=rows[:].indirect(offsets[:]), func=COPY, scale=gain[:, t : t + 1]
            )
            return fetched

        w2_dealt_words = deal_words("w2", w2_tile)
        w_dealt_words = deal_words("w", w_tile)
        first, second, third, last = ORDER
        half_slots = [slice(J // 2 * half, J // 2 * (half + 1)) for half in range(2)]

        def gather_slots(picked, window, offsets, slots):
            nc.vector.tensor_copy(picked[:, slots], window[:].indirect(offsets[:, slots.start // 16 : slots.stop // 16]))

        xo_picked = sbuf("xo_picked", J, U16)
        xo_picked_scales = sbuf("xo_picked_scales", J, U8)
        b_rows = {t: sbuf("b%d" % t, J, F32) for t in ORDER}
        w2_dealt = (w2_dealt_words, deal_scales("w2", w2_plane))
        for slots in half_slots:
            gather_slots(xo_picked, xo_tile, list2, slots)
            gather_slots(xo_picked_scales, xo_plane, list2, slots)
        for slots in half_slots:
            for t in ORDER:
                bank = product(t, w2_dealt, xo_picked[:, slots], xo_picked_scales[:, slots])
                leave_bank(b_rows[t][:, slots], bank, True)
        w_dealt = (w_dealt_words, deal_scales("w", w_plane))
        xt_picked = gather("xt_picked", xt_tile, list1, J, U16)
        xt_picked_scales = sbuf("xt_picked_scales", J, U8)
        for slots in half_slots:
            gather_slots(xt_picked_scales, xt_plane, list1, slots)
        b_fetched = {t: fetch("bf%d" % t, b_rows[t], list4, gain_b, t) for t in ORDER}
        a_rows = {t: sbuf("a%d" % t, J, F32) for t in ORDER}
        for slots in half_slots:
            bank = product(first, w_dealt, xt_picked[:, slots], xt_picked_scales[:, slots])
            leave_bank(a_rows[first][:, slots], bank, False)
        for t in (second, third, last):
            leave_bank(a_rows[t][:], product(t, w_dealt, xt_picked[:], xt_picked_scales[:]), False)
        a_fetched = {t: fetch("af%d" % t, a_rows[t], list3, gain_a, t) for t in ORDER}
        page = {}
        for t in ORDER:
            page[t] = sbuf("page%d" % t, C, F32, "a%d" % t)
            nc.gpsimd.memset(page[t][:], 0.0)

        def put(t, tag):
            larger = sbuf("larger%d" % t, S, F32, tag)
            nc.vector.tensor_tensor(larger[:], a_fetched[t][:], b_fetched[t][:], MAX)
            nc.scalar.activation(out=page[t][:].indirect(list5[:]), in_=larger[:], func=COPY)

        for t in (first, second, third):
            put(t, None)
        vs_picked_scales = gather("vs_picked_scales", vs_plane, list6, N, U8, "af%d" % third)
        vs_picked = gather("vs_picked", vs_tile, list6, N, U32, "vs_plane")
        woven = keep.tile([P, C, PACK], BF16, name="woven", tag="vs_tile", align_bytes=64)
        nc.vector.tensor_copy(out=woven[:, :, first], in_=page[first][:])
        put(last, "a%d" % first)
        for t in (second, third):
            nc.vector.tensor_copy(out=woven[:, :, t], in_=page[t][:])

        codes = sbuf("codes", C, U32)
        code_scales = sbuf("code_scales", C, U8)

        def weave_last(h):
            cols = slice(PIECE * h, PIECE * (h + 1))
            if h < PIECES // 2:
                nc.vector.tensor_copy(out=woven[:, cols, PACK - 1], in_=page[PACK - 1][:, cols])
            else:
                nc.scalar.copy(out=woven[:, cols, PACK - 1], in_=page[PACK - 1][:, cols])

        def finish(h):
            cols = slice(PIECE * h, PIECE * (h + 1))
            nc.vector.quantize_mx(
                out=codes[:, cols].bitcast(FP8X4), scales=code_scales[:, cols],
                in_=woven[:, cols, :].rearrange("p c t -> p (c t)"),
            )
            bank = psum.tile([P, N // P, PIECE], F32, name="bank")
            for m in range(N // P):
                rows = slice(P * m, P * (m + 1))
                nc.tensor.matmul_mx(
                    out=bank[:, m, :], lhsT=vs_picked[:, rows].bitcast(FP8X4), lhsT_scale=vs_picked_scales[:, rows],
                    rhs=codes[:, cols].bitcast(FP8X4), rhs_scale=code_scales[:, cols], start=True, stop=True,
                )
            return bank

        def store(h, bank):
            cols = slice(PIECE * h, PIECE * (h + 1))
            result = keep.tile([P, N // P, PIECE], F32, name="result%d" % h)
            leave_bank(result[:], bank, h < PIECES - 1)
            nc.sync.dma_start(out=out[:, cols].rearrange("(m p) c -> p m c", p=P), in_=result[:])

        weave_last(0)
        banks = []
        for h in range(PIECES):
            if h + 1 < PIECES:
                weave_last(h + 1)
            banks.append(finish(h))
        for h in range(PIECES):
            store(h, banks[h])
